import numpy as np
import ml_dtypes


def mxq(x, axis, fmt="e4m3"):
    dtype, down = {"e4m3": (ml_dtypes.float8_e4m3fn, 7), "e5m2": (ml_dtypes.float8_e5m2, 14)}[fmt]
    v = np.moveaxis(np.asarray(x, np.float32).astype(ml_dtypes.bfloat16).astype(np.float64), axis, -1)
    blocks = v.reshape(v.shape[:-1] + (-1, 32))
    amax = np.abs(blocks).max(-1, keepdims=True)
    byte = np.maximum(np.where(amax > 0, np.frexp(amax)[1] - 1 + 127, 0) - down, 1)
    scale = np.exp2(byte - 127.0)
    codes = (blocks / scale).astype(np.float32).astype(dtype).astype(np.float64)
    return np.moveaxis((codes * scale).reshape(v.shape), -1, axis)


WIDE = False


def mx_kscale(k):
    if not WIDE:
        return np.ones(k)
    levels = np.array([24, -24, 12, -12, 0])
    if k % 512:
        return np.exp2(np.random.permutation(np.resize(levels, k // 32))).repeat(32)
    a = np.empty((k // 512, 16))
    for p in range(k // 512):
        a[p, :8] = np.random.permutation(np.resize(levels, 8))
        for g in range(8):
            far = levels[np.abs(levels - a[p, g]) >= 10]
            a[p, g + 8] = far[np.random.randint(len(far))]
    return np.exp2(a.ravel()).repeat(32)


def f64(x):
    return np.asarray(x).astype(np.float64)


def striped8(idx):
    return np.concatenate([v.reshape(-1, 16).T for v in idx]).astype(np.uint16)


def unstriped8(offs):
    return np.stack([offs[16 * g:16 * g + 16].T.reshape(-1) for g in range(8)]).astype(np.int64)


E2M1 = np.array([0.0, 0.5, 1.0, 1.5, 2.0, 3.0, 4.0, 6.0, -0.0, -0.5, -1.0, -1.5, -2.0, -3.0, -4.0, -6.0])


def pack_weight(w, fmt):
    k, n = w.shape
    w = f64(np.asarray(w, np.float32).astype(ml_dtypes.bfloat16)).reshape(k // 32, 32, n)
    amax = np.abs(w).max(1)
    if fmt == "e4m3":
        byte = np.frexp(amax)[1] - 1 + 127 - 7
    else:
        mant, ex = np.frexp(amax / 6.0)
        byte = np.where(mant > 0.5, ex, ex - 1) + 127
    byte = np.clip(np.where(amax > 0, byte, 1), 1, 254)
    scaled = (w * np.exp2(127.0 - byte)[:, None, :]).reshape(k, n).astype(np.float32)
    by_word = np.ascontiguousarray(scaled.reshape(k // 512, 128, 4, n).transpose(0, 1, 3, 2))
    if fmt == "e4m3":
        words = by_word.astype(ml_dtypes.float8_e4m3fn).view(np.uint8)
    else:
        c = by_word.astype(ml_dtypes.float4_e2m1fn).view(np.uint8) & 0xF
        words = (c[..., 0::2] | (c[..., 1::2] << 4)).reshape(k // 512, 128, 2 * n)
    return np.ascontiguousarray(words), np.ascontiguousarray(byte.astype(np.uint8).reshape(k // 512, 16, n))


def unpack_weight(words, scales, fmt):
    g, _, n = scales.shape
    words = np.ascontiguousarray(words).reshape(g, 128, n, -1)
    if fmt == "e4m3":
        vals = words.view(ml_dtypes.float8_e4m3fn).astype(np.float64)
    else:
        nib = np.empty((g, 128, n, 4), np.uint8)
        nib[..., 0::2] = words & 0xF
        nib[..., 1::2] = words >> 4
        vals = E2M1[nib]
    vals = vals * np.repeat(np.exp2(scales.astype(np.float64) - 127.0), 8, axis=1)[..., None]
    return vals.transpose(0, 1, 3, 2).reshape(g * 512, n)


def planes(y):
    n, m = y.shape
    v = y.astype(np.float32).astype(ml_dtypes.bfloat16).astype(np.float64).reshape(n // 32, 32, m)
    top = np.abs(v).max(1)
    byte = np.clip(np.where(top > 0, np.frexp(top)[1] - 1 + 127 - 7, 1), 1, 254)
    codes = (v * np.exp2(127.0 - byte)[:, None, :]).reshape(n, m).astype(np.float32).astype(ml_dtypes.float8_e4m3fn).view(np.uint8)
    words = codes.reshape(n // 512, 128, 4, m).transpose(0, 1, 3, 2)
    return np.ascontiguousarray(words), np.ascontiguousarray(byte.astype(np.uint8).reshape(n // 512, 16, m))


K, L, N, T, J = 1024, 512, 512, 2048, 1024


def setup_inputs():
    n = np.random.standard_normal
    s = mx_kscale(K)[:, None]
    s2 = mx_kscale(L)[:, None]
    p_wx = pack_weight(n((L, N)) / np.sqrt(L) / s2, "e2m1")
    return {
        "xT": (n((K, T)) * s).astype(np.float32),
        "wgt": np.repeat(np.random.uniform(0.5, 2.0, (8, J)), 16, axis=0).astype(np.float32),
        "wt": (n((K, N)) / np.sqrt(K) / s).astype(np.float32),
        "c": (n((L, J)) * s2).astype(np.float32),
        "wx_words": p_wx[0],
        "wx_scales": p_wx[1],
        "offs": striped8(np.stack([np.random.permutation(T)[:J] for _ in range(8)])),
    }


def reference(xT, wgt, wt, c, wx_words, wx_scales, offs):
    idx = unstriped8(offs)
    rows = np.arange(K)
    xg = f64(wgt)[rows // 4 % 128] * f64(xT)[rows[:, None], idx[rows % 512 // 64]]
    xT_ = mxq(xg, 0, "e4m3")
    wt_ = mxq(f64(wt), 0, "e4m3")
    c_q_ = mxq(f64(c), 0, "e4m3")
    c_r_ = mxq(f64(c) - c_q_, 0, "e4m3")
    wx_ = unpack_weight(wx_words, wx_scales, "e2m1")
    y = wt_.T @ xT_ + wx_.T @ c_q_ + wx_.T @ c_r_
    return (y,) + planes(y)

@@ -1,0 +1,263 @@
+from contextlib import ExitStack
+
+import concourse.mybir as mybir
+from concourse.masks import make_identity
+
+K, L, N, T, J = 1024, 512, 512, 2048, 1024
+FLOPS = 2 * (K * N * J + 2 * L * N * J + L * L * J)
+
+F32 = mybir.dt.float32
+BF16 = mybir.dt.bfloat16
+I32 = mybir.dt.int32
+U32 = mybir.dt.uint32
+U16 = mybir.dt.uint16
+U8 = mybir.dt.uint8
+FP8X4 = mybir.dt.float8_e4m3fn_x4
+FP4X4 = mybir.dt.float4_e2m1fn_x4
+MULT = mybir.AluOpType.mult
+SUB = mybir.AluOpType.subtract
+
+P = 128
+PACK = 4
+BANK = 128
+HALF = 512
+QUARTER = 256
+
+
+def tile_list_noneP_kernel(
+    tc, xT, wgt, wt, c, wx_words, wx_scales, offs, out_0, out_1, out_2
+):
+    nc = tc.nc
+    with ExitStack() as ctx:
+        sb = ctx.enter_context(tc.tile_pool(name="sb", bufs=1))
+        ps = ctx.enter_context(tc.psum_pool(name="ps", bufs=1))
+
+        def tile(name, shape, dtype):
+            return sb.tile(shape, dtype, name=name, align_bytes=64)
+
+        def quantize(codes, scales, grouped):
+            nc.vector.quantize_mx(
+                out=codes.bitcast(FP8X4), scales=scales, in_=grouped.rearrange("p w i -> p (w i)")
+            )
+
+        def interleave(copy, grouped, planes):
+            copy(
+                grouped.rearrange("p (g e) i -> p g i e", e=4),
+                planes.rearrange("p i (g e) -> p g i e", e=4),
+            )
+
+        x_rows = xT.rearrange("(a p i) t -> a i p t", p=P, i=PACK)
+        wt_rows = wt.rearrange("(a p i) n -> a p i n", p=P, i=PACK)
+        c_rows = c.rearrange("(p i) j -> p i j", i=PACK)
+        y_rows = out_0.rearrange("(p i) j -> p i j", i=PACK)
+        y_words = out_1[0].rearrange("p j i -> p (j i)")
+
+        offsets = tile("offsets", [P, J // 16], U16)
+        c_sb = [tile("c%d" % h, [P, PACK, HALF], F32) for h in range(2)]
+        wgt_sb = tile("wgt", [P, J], F32)
+        x_sb = [tile("x%d" % n, [P, T], F32) for n in range(8)]
+        wt_sb = [tile("wt%d" % a, [P, PACK, N], F32) for a in range(2)]
+        wx_raw = tile("wx_raw", [P, 2 * N], U8)
+        wxs_raw = tile("wxs_raw", [P, N], U8)
+
+        def load_x(n):
+            nc.sync.dma_start(x_sb[n][:], x_rows[n // PACK, n % PACK])
+
+        def load_c(h):
+            nc.sync.dma_start(c_sb[h][:], c_rows[:, :, h * HALF : (h + 1) * HALF])
+
+        def load_wgt(h):
+            nc.sync.dma_start(wgt_sb[:, h * HALF : (h + 1) * HALF], wgt[:, h * HALF : (h + 1) * HALF])
+
+        def load_wt(a):
+            nc.sync.dma_start(wt_sb[a][:], wt_rows[a])
+
+        nc.vector.memset(wxs_raw[:].bitcast(I32), 0)
+        nc.sync.dma_start(offsets[:], offs)
+        load_c(0)
+        nc.scalar.dma_start(wx_raw[:].bitcast(I32), wx_words[0].bitcast(I32))
+        for q in range(4):
+            nc.scalar.dma_start(
+                wxs_raw[32 * q : 32 * q + 4, :].bitcast(I32), wx_scales[0, 4 * q : 4 * q + 4, :].bitcast(I32)
+            )
+        load_wgt(0)
+        load_x(0)
+        load_wgt(1)
+        load_x(1)
+        load_c(1)
+        load_x(2)
+        load_wt(0)
+        load_x(3)
+        load_x(4)
+        load_x(5)
+        load_wt(1)
+        load_x(6)
+        load_x(7)
+
+        eye = tile("eye", [P, P], BF16)
+        make_identity(nc, eye[:])
+        eye_grouped = tile("eye_grouped", [P, PACK * P, PACK], BF16)
+        nc.vector.memset(eye_grouped[:], 0.0)
+        for t in range(PACK):
+            nc.vector.tensor_copy(eye_grouped[:, t * P : (t + 1) * P, t], eye[:])
+        eye_codes = tile("eye_codes", [P, PACK * P], U32)
+        eye_scales = tile("eye_scales", [P, PACK * P], U8)
+        quantize(eye_codes[:], eye_scales[:], eye_grouped[:])
+
+        wx_codes = tile("wx_codes", [P, 2 * N], U8)
+        wx_sc = tile("wx_sc", [P, N], U8)
+        nc.vector.tensor_copy(
+            wx_codes[:].rearrange("p (t m b) -> p m t b", t=PACK, b=2),
+            wx_raw[:].rearrange("p (m t b) -> p m t b", t=PACK, b=2),
+        )
+        nc.vector.tensor_copy(
+            wx_sc[:].rearrange("p (t m) -> p m t", t=PACK),
+            wxs_raw[:].rearrange("p (m t) -> p m t", t=PACK),
+        )
+
+        cq_codes = [tile("cq_codes%d" % q, [P, QUARTER], U32) for q in range(4)]
+        cq_scales = [tile("cq_scales%d" % q, [P, QUARTER], U8) for q in range(4)]
+        cr_codes = [tile("cr_codes%d" % q, [P, QUARTER], U32) for q in range(4)]
+        cr_scales = [tile("cr_scales%d" % q, [P, QUARTER], U8) for q in range(4)]
+        y_ps = {}
+
+        def mx(out, w_codes, w_scales, m_codes, m_scales, start, stop):
+            nc.tensor.matmul_mx(
+                out=out, lhsT=w_codes, lhsT_scale=w_scales, rhs=m_codes.bitcast(FP8X4), rhs_scale=m_scales,
+                start=start, stop=stop,
+            )
+
+        def wx_passes(b, codes, scales, first):
+            cols = slice((b % 2) * BANK, (b % 2 + 1) * BANK)
+            for t in range(PACK):
+                mx(y_ps[b][:, t, :], wx_codes[:, 2 * P * t : 2 * P * (t + 1)].bitcast(FP4X4),
+                   wx_sc[:, P * t : P * (t + 1)], codes[:, cols], scales[:, cols], first and t == 0, False)
+
+        def c_first_tier(q):
+            grouped = tile("c_grouped%d" % q, [P, QUARTER, PACK], BF16)
+            src = c_sb[q // 2][:, :, (q % 2) * QUARTER : (q % 2 + 1) * QUARTER]
+            interleave(nc.scalar.copy, grouped[:], src)
+            quantize(cq_codes[q][:], cq_scales[q][:], grouped[:])
+
+        def c_second_tier(q):
+            left = tile("left_grouped%d" % q, [P, QUARTER, PACK], BF16)
+            for u in range(2):
+                b = 2 * q + u
+                cols = slice(u * BANK, (u + 1) * BANK)
+                back = ps.tile([P, PACK, BANK], F32, name="back%d" % b, tag="bank%d" % b)
+                for t in range(PACK):
+                    mx(back[:, t, :], eye_codes[:, P * t : P * (t + 1)].bitcast(FP8X4),
+                       eye_scales[:, P * t : P * (t + 1)], cq_codes[q][:, cols], cq_scales[q][:, cols], True, True)
+                j0 = (b % 4) * BANK
+                nc.vector.tensor_tensor(
+                    left[:, cols, :].rearrange("p (g e) i -> p g i e", e=2),
+                    c_sb[q // 2][:, :, j0 : j0 + BANK].rearrange("p i (g e) -> p g i e", e=2),
+                    back[:].rearrange("p i (g e) -> p g i e", e=2),
+                    SUB,
+                )
+                y_ps[b] = ps.tile([P, PACK, BANK], F32, name="y%d" % b, tag="bank%d" % b)
+                wx_passes(b, cq_codes[q], cq_scales[q], True)
+            quantize(cr_codes[q][:], cr_scales[q][:], left[:])
+            for u in range(2):
+                wx_passes(2 * q + u, cr_codes[q], cr_scales[q], False)
+
+        picked0 = tile("picked0all", [P, PACK, J], F32)
+        picked1 = [tile("picked1_%d" % u, [P, 2, J], F32) for u in range(2)]
+
+        def gather(n, j0, j1):
+            dst = picked0[:, n, j0:j1] if n < PACK else picked1[(n - PACK) // 2][:, n % 2, j0:j1]
+            nc.vector.tensor_tensor(
+                dst, x_sb[n][:].indirect(offsets[:, j0 // 16 : j1 // 16]), wgt_sb[:, j0:j1], MULT
+            )
+
+        wt_codes = [tile("wt_codes%d" % a, [P, N], U32) for a in range(2)]
+        wt_scales = [tile("wt_scales%d" % a, [P, N], U8) for a in range(2)]
+
+        def quantize_wt(a):
+            grouped = tile("wt_grouped%d" % a, [P, N, PACK], BF16)
+            nc.scalar.copy(
+                grouped[:].rearrange("p (t m) i -> p m i t", t=PACK),
+                wt_sb[a][:].rearrange("p i (m t) -> p m i t", t=PACK),
+            )
+            quantize(wt_codes[a][:], wt_scales[a][:], grouped[:])
+
+        def wt_passes(a, b, codes, scales, last):
+            for t in range(PACK):
+                mx(y_ps[b][:, t, :], wt_codes[a][:, P * t : P * (t + 1)].bitcast(FP8X4),
+                   wt_scales[a][:, P * t : P * (t + 1)], codes, scales, False, last and t == PACK - 1)
+
+        c_first_tier(0)
+        c_first_tier(1)
+        c_second_tier(0)
+        c_second_tier(1)
+        gather(0, 0, HALF)
+        gather(0, HALF, J)
+        gather(1, 0, J)
+        c_first_tier(2)
+        c_first_tier(3)
+        c_second_tier(2)
+        gather(2, 0, J)
+        c_second_tier(3)
+        quantize_wt(0)
+        gather(3, 0, HALF)
+        gather(3, HALF, J)
+        gather(4, 0, J)
+        for h in range(2):
+            grouped = tile("xg0_grouped%d" % h, [P, HALF, PACK], BF16)
+            interleave(nc.scalar.copy, grouped[:], picked0[:, :, h * HALF : (h + 1) * HALF])
+            codes = tile("xg0_codes%d" % h, [P, HALF], U32)
+            scales = tile("xg0_scales%d" % h, [P, HALF], U8)
+            quantize(codes[:], scales[:], grouped[:])
+            for u in range(4):
+                cols = slice(u * BANK, (u + 1) * BANK)
+                wt_passes(0, 4 * h + u, codes[:, cols], scales[:, cols], False)
+        gather(5, 0, J)
+        xg1_grouped = [tile("xg1_grouped%d" % q, [P, QUARTER, PACK], BF16) for q in range(4)]
+
+        def round_pair(u, q):
+            nc.scalar.copy(
+                xg1_grouped[q][:, :, 2 * u : 2 * u + 2],
+                picked1[u][:, :, q * QUARTER : (q + 1) * QUARTER].rearrange("p e j -> p j e"),
+            )
+
+        quantize_wt(1)
+        for q in range(4):
+            round_pair(0, q)
+        gather(6, 0, J)
+
+        y_scales = tile("y_scales", [P, J], U8)
+        y_sb = [tile("y_sb%d" % q, [P, PACK, QUARTER], F32) for q in range(4)]
+
+        def last_passes(q):
+            gather(7, q * QUARTER, (q + 1) * QUARTER)
+            round_pair(1, q)
+            codes = tile("xg1_codes%d" % q, [P, QUARTER], U32)
+            scales = tile("xg1_scales%d" % q, [P, QUARTER], U8)
+            quantize(codes[:], scales[:], xg1_grouped[q][:])
+            for u in range(2):
+                cols = slice(u * BANK, (u + 1) * BANK)
+                wt_passes(1, 2 * q + u, codes[:, cols], scales[:, cols], True)
+
+        def hand_out(q):
+            js = slice(q * QUARTER, (q + 1) * QUARTER)
+            for u in range(2):
+                nc.scalar.copy(y_sb[q][:, :, u * BANK : (u + 1) * BANK], y_ps[2 * q + u][:])
+            nc.sync.dma_start(y_rows[:, :, js], y_sb[q][:])
+            grouped = tile("y_grouped%d" % q, [P, QUARTER, PACK], BF16)
+            interleave(nc.vector.tensor_copy, grouped[:], y_sb[q][:])
+            codes = tile("y_codes%d" % q, [P, QUARTER], U32)
+            quantize(codes[:], y_scales[:, js], grouped[:])
+            nc.sync.dma_start(
+                y_words[:, PACK * q * QUARTER : PACK * (q + 1) * QUARTER].bitcast(I32), codes[:].bitcast(I32)
+            )
+
+        last_passes(0)
+        for q in range(1, 4):
+            last_passes(q)
+            hand_out(q - 1)
+        hand_out(3)
+        for q in range(4):
+            queue = nc.sync if q % 2 == 0 else nc.scalar
+            queue.dma_start(
+                out_2[0, 4 * q : 4 * q + 4, :].bitcast(I32), y_scales[32 * q : 32 * q + 4, :].bitcast(I32)
+            )

@@ -32,8 +32,8 @@ def tile_list_noneP_kernel(
         sb = ctx.enter_context(tc.tile_pool(name="sb", bufs=1))
         ps = ctx.enter_context(tc.psum_pool(name="ps", bufs=1))
 
-        def tile(name, shape, dtype):
-            return sb.tile(shape, dtype, name=name, align_bytes=64)
+        def tile(name, shape, dtype, tag=None):
+            return sb.tile(shape, dtype, name=name, tag=tag or name, align_bytes=64)
 
         def quantize(codes, scales, grouped):
             nc.vector.quantize_mx(
@@ -53,7 +53,8 @@ def tile_list_noneP_kernel(
         y_words = out_1[0].rearrange("p j i -> p (j i)")
 
         offsets = tile("offsets", [P, J // 16], U16)
-        c_sb = [tile("c%d" % h, [P, PACK, HALF], F32) for h in range(2)]
+        c_all = tile("c_all", [P, PACK * J], F32)
+        c_sb = [c_all[:, q * J : (q + 1) * J].rearrange("p (i j) -> p i j", i=PACK) for q in range(4)]
         wgt_sb = tile("wgt", [P, J], F32)
         x_sb = [tile("x%d" % n, [P, T], F32) for n in range(8)]
         wt_sb = [tile("wt%d" % a, [P, PACK, N], F32) for a in range(2)]
@@ -63,56 +64,45 @@ def tile_list_noneP_kernel(
         def load_x(n):
             nc.sync.dma_start(x_sb[n][:], x_rows[n // PACK, n % PACK])
 
-        def load_c(h):
-            nc.sync.dma_start(c_sb[h][:], c_rows[:, :, h * HALF : (h + 1) * HALF])
-
-        def load_wgt(h):
-            nc.sync.dma_start(wgt_sb[:, h * HALF : (h + 1) * HALF], wgt[:, h * HALF : (h + 1) * HALF])
+        def load_c(q):
+            nc.sync.dma_start(c_sb[q], c_rows[:, :, q * QUARTER : (q + 1) * QUARTER])
 
         def load_wt(a):
             nc.sync.dma_start(wt_sb[a][:], wt_rows[a])
 
-        nc.vector.memset(wxs_raw[:].bitcast(I32), 0)
-        nc.sync.dma_start(offsets[:], offs)
-        load_c(0)
-        nc.scalar.dma_start(wx_raw[:].bitcast(I32), wx_words[0].bitcast(I32))
+        nc.sync.dma_start(wx_raw[:].bitcast(I32), wx_words[0].bitcast(I32))
         for q in range(4):
-            nc.scalar.dma_start(
-                wxs_raw[32 * q : 32 * q + 4, :].bitcast(I32), wx_scales[0, 4 * q : 4 * q + 4, :].bitcast(I32)
-            )
-        load_wgt(0)
+            load_c(q)
+        nc.sync.dma_start(offsets[:], offs)
+        nc.sync.dma_start(wgt_sb[:], wgt)
         load_x(0)
-        load_wgt(1)
+        for q in range(4):
+            rows = wx_scales[:, 4 * q : 4 * q + 4, :].bitcast(I32)
+            nc.sync.dma_start(wxs_raw[32 * q : 32 * (q + 1), :].bitcast(I32), rows.broadcast_to([8, 4, N // 4]))
         load_x(1)
-        load_c(1)
-        load_x(2)
         load_wt(0)
+        load_x(2)
+        load_wt(1)
         load_x(3)
         load_x(4)
         load_x(5)
-        load_wt(1)
         load_x(6)
         load_x(7)
 
         eye = tile("eye", [P, P], BF16)
         make_identity(nc, eye[:])
-        eye_grouped = tile("eye_grouped", [P, PACK * P, PACK], BF16)
-        nc.vector.memset(eye_grouped[:], 0.0)
-        for t in range(PACK):
-            nc.vector.tensor_copy(eye_grouped[:, t * P : (t + 1) * P, t], eye[:])
+        eye_grouped = tile("eye_grouped", [P, PACK, PACK * P + 1], BF16)
+        eye_flat = eye_grouped[:].rearrange("p t w -> p (t w)")
+        nc.vector.memset(eye_flat, 0.0)
+        nc.scalar.copy(eye_grouped[:, :, 0 : PACK * P : PACK], eye[:].unsqueeze(1).broadcast_to([P, PACK, P]))
         eye_codes = tile("eye_codes", [P, PACK * P], U32)
         eye_scales = tile("eye_scales", [P, PACK * P], U8)
-        quantize(eye_codes[:], eye_scales[:], eye_grouped[:])
+        nc.vector.quantize_mx(out=eye_codes[:].bitcast(FP8X4), scales=eye_scales[:], in_=eye_flat[:, 0 : PACK * PACK * P])
 
         wx_codes = tile("wx_codes", [P, 2 * N], U8)
-        wx_sc = tile("wx_sc", [P, N], U8)
         nc.vector.tensor_copy(
-            wx_codes[:].rearrange("p (t m b) -> p m t b", t=PACK, b=2),
-            wx_raw[:].rearrange("p (m t b) -> p m t b", t=PACK, b=2),
-        )
-        nc.vector.tensor_copy(
-            wx_sc[:].rearrange("p (t m) -> p m t", t=PACK),
-            wxs_raw[:].rearrange("p (m t) -> p m t", t=PACK),
+            wx_codes[:].bitcast(U16).rearrange("p (t m) -> p t m", t=PACK),
+            wx_raw[:].bitcast(U16).rearrange("p (m t) -> p t m", t=PACK),
         )
 
         cq_codes = [tile("cq_codes%d" % q, [P, QUARTER], U32) for q in range(4)]
@@ -127,48 +117,56 @@ def tile_list_noneP_kernel(
                 start=start, stop=stop,
             )
 
-        def wx_passes(b, codes, scales, first):
-            cols = slice((b % 2) * BANK, (b % 2 + 1) * BANK)
-            for t in range(PACK):
-                mx(y_ps[b][:, t, :], wx_codes[:, 2 * P * t : 2 * P * (t + 1)].bitcast(FP4X4),
-                   wx_sc[:, P * t : P * (t + 1)], codes[:, cols], scales[:, cols], first and t == 0, False)
+        def wx_passes(q, wx_sc):
+            for codes, scales, first in ((cq_codes[q], cq_scales[q], True), (cr_codes[q], cr_scales[q], False)):
+                for u in range(2):
+                    b = 2 * q + u
+                    cols = slice(u * BANK, (u + 1) * BANK)
+                    if first:
+                        y_ps[b] = ps.tile([P, PACK, BANK], F32, name="y%d" % b, tag="bank%d" % b)
+                    for t in range(PACK):
+                        mx(y_ps[b][:, t, :], wx_codes[:, 2 * P * t : 2 * P * (t + 1)].bitcast(FP4X4),
+                           wx_sc[:, P * t : P * (t + 1)], codes[:, cols], scales[:, cols], first and t == 0, False)
+
+        back = {}
+
+        c_grouped = tile("c_grouped", [P, J, PACK], BF16, tag="eye_grouped")
 
         def c_first_tier(q):
-            grouped = tile("c_grouped%d" % q, [P, QUARTER, PACK], BF16)
-            src = c_sb[q // 2][:, :, (q % 2) * QUARTER : (q % 2 + 1) * QUARTER]
-            interleave(nc.scalar.copy, grouped[:], src)
-            quantize(cq_codes[q][:], cq_scales[q][:], grouped[:])
-
-        def c_second_tier(q):
-            left = tile("left_grouped%d" % q, [P, QUARTER, PACK], BF16)
+            grouped = c_grouped[:, q * QUARTER : (q + 1) * QUARTER, :]
+            interleave(nc.scalar.copy, grouped, c_sb[q])
+            quantize(cq_codes[q][:], cq_scales[q][:], grouped)
             for u in range(2):
                 b = 2 * q + u
                 cols = slice(u * BANK, (u + 1) * BANK)
-                back = ps.tile([P, PACK, BANK], F32, name="back%d" % b, tag="bank%d" % b)
+                back[b] = ps.tile([P, PACK, BANK], F32, name="back%d" % b, tag="bank%d" % b)
                 for t in range(PACK):
-                    mx(back[:, t, :], eye_codes[:, P * t : P * (t + 1)].bitcast(FP8X4),
+                    mx(back[b][:, t, :], eye_codes[:, P * t : P * (t + 1)].bitcast(FP8X4),
                        eye_scales[:, P * t : P * (t + 1)], cq_codes[q][:, cols], cq_scales[q][:, cols], True, True)
-                j0 = (b % 4) * BANK
+
+        left = {}
+
+        def leftover(q):
+            left[q] = tile("left_grouped%d" % q, [P, QUARTER, PACK], BF16)
+            for u in range(2):
+                cols = slice(u * BANK, (u + 1) * BANK)
                 nc.vector.tensor_tensor(
-                    left[:, cols, :].rearrange("p (g e) i -> p g i e", e=2),
-                    c_sb[q // 2][:, :, j0 : j0 + BANK].rearrange("p i (g e) -> p g i e", e=2),
-                    back[:].rearrange("p i (g e) -> p g i e", e=2),
+                    left[q][:, cols, :].rearrange("p (g e) i -> p g i e", e=4),
+                    c_sb[q][:, :, cols].rearrange("p i (g e) -> p g i e", e=4),
+                    back[2 * q + u][:].rearrange("p i (g e) -> p g i e", e=4),
                     SUB,
                 )
-                y_ps[b] = ps.tile([P, PACK, BANK], F32, name="y%d" % b, tag="bank%d" % b)
-                wx_passes(b, cq_codes[q], cq_scales[q], True)
-            quantize(cr_codes[q][:], cr_scales[q][:], left[:])
-            for u in range(2):
-                wx_passes(2 * q + u, cr_codes[q], cr_scales[q], False)
 
-        picked0 = tile("picked0all", [P, PACK, J], F32)
-        picked1 = [tile("picked1_%d" % u, [P, 2, J], F32) for u in range(2)]
+        def c_second_tier(q):
+            quantize(cr_codes[q][:], cr_scales[q][:], left[q][:])
 
-        def gather(n, j0, j1):
-            dst = picked0[:, n, j0:j1] if n < PACK else picked1[(n - PACK) // 2][:, n % 2, j0:j1]
+        def gather(n, j0, j1, dst):
             nc.vector.tensor_tensor(
                 dst, x_sb[n][:].indirect(offsets[:, j0 // 16 : j1 // 16]), wgt_sb[:, j0:j1], MULT
             )
+
+        def round_pair(grouped, u, src):
+            nc.scalar.copy(grouped[:, :, 2 * u : 2 * u + 2], src.rearrange("p e j -> p j e"))
 
         wt_codes = [tile("wt_codes%d" % a, [P, N], U32) for a in range(2)]
         wt_scales = [tile("wt_scales%d" % a, [P, N], U8) for a in range(2)]
@@ -187,50 +185,57 @@ def tile_list_noneP_kernel(
                    wt_scales[a][:, P * t : P * (t + 1)], codes, scales, False, last and t == PACK - 1)
 
         c_first_tier(0)
-        c_first_tier(1)
-        c_second_tier(0)
-        c_second_tier(1)
-        gather(0, 0, HALF)
-        gather(0, HALF, J)
-        gather(1, 0, J)
-        c_first_tier(2)
-        c_first_tier(3)
-        c_second_tier(2)
-        gather(2, 0, J)
+        for q in range(1, 4):
+            c_first_tier(q)
+            leftover(q - 1)
+            c_second_tier(q - 1)
+        leftover(3)
         c_second_tier(3)
-        quantize_wt(0)
-        gather(3, 0, HALF)
-        gather(3, HALF, J)
-        gather(4, 0, J)
+        picked0 = tile("picked0", [P, PACK, J], F32, tag="c_all")
+        gather(0, 0, J, picked0[:, 0, :])
+        wx_sc = tile("wx_sc", [P, N], U8, tag="left_grouped3")
+        nc.vector.tensor_copy(
+            wx_sc[:].rearrange("p (t m) -> p t m", t=PACK),
+            wxs_raw[:].rearrange("p (m t) -> p t m", t=PACK),
+        )
+        for q in range(4):
+            wx_passes(q, wx_sc)
+        gather(1, 0, J, picked0[:, 1, :])
+        xg0_grouped = [tile("xg0_grouped%d" % h, [P, HALF, PACK], BF16) for h in range(2)]
         for h in range(2):
-            grouped = tile("xg0_grouped%d" % h, [P, HALF, PACK], BF16)
-            interleave(nc.scalar.copy, grouped[:], picked0[:, :, h * HALF : (h + 1) * HALF])
+            round_pair(xg0_grouped[h], 0, picked0[:, 0:2, h * HALF : (h + 1) * HALF])
+        gather(2, 0, J, picked0[:, 2, :])
+        quantize_wt(0)
+        gather(3, 0, J, picked0[:, 3, :])
+        quantize_wt(1)
+        for h in range(2):
+            round_pair(xg0_grouped[h], 1, picked0[:, 2:4, h * HALF : (h + 1) * HALF])
+        picked1 = tile("picked1", [P, 2, J], F32)
+        gather(4, 0, J, picked1[:, 0, :])
+
+        def first_passes(h):
             codes = tile("xg0_codes%d" % h, [P, HALF], U32)
             scales = tile("xg0_scales%d" % h, [P, HALF], U8)
-            quantize(codes[:], scales[:], grouped[:])
+            quantize(codes[:], scales[:], xg0_grouped[h][:])
             for u in range(4):
                 cols = slice(u * BANK, (u + 1) * BANK)
                 wt_passes(0, 4 * h + u, codes[:, cols], scales[:, cols], False)
-        gather(5, 0, J)
+
+        first_passes(0)
+        gather(5, 0, J, picked1[:, 1, :])
+        first_passes(1)
         xg1_grouped = [tile("xg1_grouped%d" % q, [P, QUARTER, PACK], BF16) for q in range(4)]
-
-        def round_pair(u, q):
-            nc.scalar.copy(
-                xg1_grouped[q][:, :, 2 * u : 2 * u + 2],
-                picked1[u][:, :, q * QUARTER : (q + 1) * QUARTER].rearrange("p e j -> p j e"),
-            )
-
-        quantize_wt(1)
         for q in range(4):
-            round_pair(0, q)
-        gather(6, 0, J)
+            round_pair(xg1_grouped[q], 0, picked1[:, :, q * QUARTER : (q + 1) * QUARTER])
 
         y_scales = tile("y_scales", [P, J], U8)
         y_sb = [tile("y_sb%d" % q, [P, PACK, QUARTER], F32) for q in range(4)]
 
         def last_passes(q):
-            gather(7, q * QUARTER, (q + 1) * QUARTER)
-            round_pair(1, q)
+            last = tile("picked_last%d" % q, [P, 2, QUARTER], F32, tag="picked_last%d" % (q % 2))
+            gather(6, q * QUARTER, (q + 1) * QUARTER, last[:, 0, :])
+            gather(7, q * QUARTER, (q + 1) * QUARTER, last[:, 1, :])
+            round_pair(xg1_grouped[q], 1, last[:])
             codes = tile("xg1_codes%d" % q, [P, QUARTER], U32)
             scales = tile("xg1_scales%d" % q, [P, QUARTER], U8)
             quantize(codes[:], scales[:], xg1_grouped[q][:])

@@ -53,8 +53,7 @@ def tile_list_noneP_kernel(
         y_words = out_1[0].rearrange("p j i -> p (j i)")
 
         offsets = tile("offsets", [P, J // 16], U16)
-        c_all = tile("c_all", [P, PACK * J], F32)
-        c_sb = [c_all[:, q * J : (q + 1) * J].rearrange("p (i j) -> p i j", i=PACK) for q in range(4)]
+        c_sb = [tile("c%d" % q, [P, PACK, QUARTER], F32) for q in range(4)]
         wgt_sb = tile("wgt", [P, J], F32)
         x_sb = [tile("x%d" % n, [P, T], F32) for n in range(8)]
         wt_sb = [tile("wt%d" % a, [P, PACK, N], F32) for a in range(2)]
@@ -65,20 +64,22 @@ def tile_list_noneP_kernel(
             nc.sync.dma_start(x_sb[n][:], x_rows[n // PACK, n % PACK])
 
         def load_c(q):
-            nc.sync.dma_start(c_sb[q], c_rows[:, :, q * QUARTER : (q + 1) * QUARTER])
+            nc.sync.dma_start(c_sb[q][:], c_rows[:, :, q * QUARTER : (q + 1) * QUARTER])
 
         def load_wt(a):
             nc.sync.dma_start(wt_sb[a][:], wt_rows[a])
 
         nc.sync.dma_start(wx_raw[:].bitcast(I32), wx_words[0].bitcast(I32))
-        for q in range(4):
-            load_c(q)
-        nc.sync.dma_start(offsets[:], offs)
-        nc.sync.dma_start(wgt_sb[:], wgt)
-        load_x(0)
+        load_c(0)
         for q in range(4):
             rows = wx_scales[:, 4 * q : 4 * q + 4, :].bitcast(I32)
             nc.sync.dma_start(wxs_raw[32 * q : 32 * (q + 1), :].bitcast(I32), rows.broadcast_to([8, 4, N // 4]))
+        load_c(1)
+        load_c(2)
+        load_c(3)
+        nc.sync.dma_start(offsets[:], offs)
+        nc.sync.dma_start(wgt_sb[:], wgt)
+        load_x(0)
         load_x(1)
         load_wt(0)
         load_x(2)
@@ -89,12 +90,12 @@ def tile_list_noneP_kernel(
         load_x(6)
         load_x(7)
 
-        eye = tile("eye", [P, P], BF16)
+        eye = tile("eye", [P, P], F32)
         make_identity(nc, eye[:])
-        eye_grouped = tile("eye_grouped", [P, PACK, PACK * P + 1], BF16)
-        eye_flat = eye_grouped[:].rearrange("p t w -> p (t w)")
-        nc.vector.memset(eye_flat, 0.0)
-        nc.scalar.copy(eye_grouped[:, :, 0 : PACK * P : PACK], eye[:].unsqueeze(1).broadcast_to([P, PACK, P]))
+        eye_flat = tile("eye_grouped", [P, PACK * (PACK * P + 1)], BF16)
+        nc.gpsimd.memset(eye_flat[:].bitcast(U32), 0)
+        diagonals = eye_flat[:].rearrange("p (t w) -> p t w", t=PACK)[:, :, 0 : PACK * P : PACK]
+        nc.scalar.copy(diagonals, eye[:].unsqueeze(1).broadcast_to([P, PACK, P]))
         eye_codes = tile("eye_codes", [P, PACK * P], U32)
         eye_scales = tile("eye_scales", [P, PACK * P], U8)
         nc.vector.quantize_mx(out=eye_codes[:].bitcast(FP8X4), scales=eye_scales[:], in_=eye_flat[:, 0 : PACK * PACK * P])
@@ -103,6 +104,11 @@ def tile_list_noneP_kernel(
         nc.vector.tensor_copy(
             wx_codes[:].bitcast(U16).rearrange("p (t m) -> p t m", t=PACK),
             wx_raw[:].bitcast(U16).rearrange("p (m t) -> p t m", t=PACK),
+        )
+        wx_sc = tile("wx_sc", [P, N], U8)
+        nc.vector.tensor_copy(
+            wx_sc[:].rearrange("p (t m) -> p t m", t=PACK),
+            wxs_raw[:].rearrange("p (m t) -> p t m", t=PACK),
         )
 
         cq_codes = [tile("cq_codes%d" % q, [P, QUARTER], U32) for q in range(4)]
@@ -118,12 +124,12 @@ def tile_list_noneP_kernel(
             )
 
         def wx_passes(q, wx_sc):
-            for codes, scales, first in ((cq_codes[q], cq_scales[q], True), (cr_codes[q], cr_scales[q], False)):
+            for codes, scales, first in ((cr_codes[q], cr_scales[q], True), (cq_codes[q], cq_scales[q], False)):
                 for u in range(2):
                     b = 2 * q + u
                     cols = slice(u * BANK, (u + 1) * BANK)
                     if first:
-                        y_ps[b] = ps.tile([P, PACK, BANK], F32, name="y%d" % b, tag="bank%d" % b)
+                        y_ps[b] = ps.tile([P, PACK, BANK], F32, name="y%d" % b, tag="bank%d" % (7 - b))
                     for t in range(PACK):
                         mx(y_ps[b][:, t, :], wx_codes[:, 2 * P * t : 2 * P * (t + 1)].bitcast(FP4X4),
                            wx_sc[:, P * t : P * (t + 1)], codes[:, cols], scales[:, cols], first and t == 0, False)
@@ -134,7 +140,7 @@ def tile_list_noneP_kernel(
 
         def c_first_tier(q):
             grouped = c_grouped[:, q * QUARTER : (q + 1) * QUARTER, :]
-            interleave(nc.scalar.copy, grouped, c_sb[q])
+            interleave(nc.scalar.copy, grouped, c_sb[q][:])
             quantize(cq_codes[q][:], cq_scales[q][:], grouped)
             for u in range(2):
                 b = 2 * q + u
@@ -147,7 +153,7 @@ def tile_list_noneP_kernel(
         left = {}
 
         def leftover(q):
-            left[q] = tile("left_grouped%d" % q, [P, QUARTER, PACK], BF16)
+            left[q] = tile("left_grouped%d" % q, [P, QUARTER, PACK], BF16)[:]
             for u in range(2):
                 cols = slice(u * BANK, (u + 1) * BANK)
                 nc.vector.tensor_tensor(
@@ -157,16 +163,44 @@ def tile_list_noneP_kernel(
                     SUB,
                 )
 
+        def leftover_on_tensor(q):
+            flat = tile("left_grouped%d" % q, [P, QUARTER * PACK], BF16)
+            left[q] = flat[:].rearrange("p (j i) -> p j i", i=PACK)
+            for u in range(2):
+                b = 2 * q + u
+                cols = slice(u * BANK, (u + 1) * BANK)
+                negated = tile("negated%d" % b, [P, PACK, BANK], F32)
+                nc.scalar.mul(negated[:], back[b][:], -1.0)
+                turned = ps.tile([P, PACK, P], F32, name="turned%d" % b, tag="bank%d" % b)
+                for t in range(PACK):
+                    nc.tensor.matmul(turned[:, t, :], lhsT=c_sb[q][:, t, cols], rhs=eye[:], is_transpose=True,
+                                     start=t == 0, stop=False)
+                for t in range(PACK):
+                    nc.tensor.matmul(turned[:, t, :], lhsT=negated[:, t, :], rhs=eye[:], is_transpose=True,
+                                     start=False, stop=t == PACK - 1)
+                rounded = tile("rounded%d" % b, [P, PACK * P], BF16)
+                nc.scalar.copy(
+                    rounded[:].rearrange("j (v p e) -> j v p e", v=2, e=2),
+                    turned[:].rearrange("j (v e) p -> j v p e", v=2),
+                )
+                pairs = ps.tile([P, 2, BANK], F32, name="pairs%d" % b, tag="bank%d" % b)
+                for v in range(2):
+                    nc.tensor.transpose(pairs[:, v, :], rounded[:].bitcast(F32)[:, v * P : (v + 1) * P], eye[:])
+                nc.scalar.copy(
+                    flat[:].bitcast(F32)[:, 2 * u * BANK : 2 * (u + 1) * BANK].rearrange("p (j v) -> p j v", v=2),
+                    pairs[:].rearrange("p v j -> p j v"),
+                )
+
         def c_second_tier(q):
-            quantize(cr_codes[q][:], cr_scales[q][:], left[q][:])
+            quantize(cr_codes[q][:], cr_scales[q][:], left[q])
 
         def gather(n, j0, j1, dst):
             nc.vector.tensor_tensor(
                 dst, x_sb[n][:].indirect(offsets[:, j0 // 16 : j1 // 16]), wgt_sb[:, j0:j1], MULT
             )
 
-        def round_pair(grouped, u, src):
-            nc.scalar.copy(grouped[:, :, 2 * u : 2 * u + 2], src.rearrange("p e j -> p j e"))
+        def round_pair(grouped, u, src, copy=nc.scalar.copy):
+            copy(grouped[:, :, 2 * u : 2 * u + 2], src.rearrange("p e j -> p j e"))
 
         wt_codes = [tile("wt_codes%d" % a, [P, N], U32) for a in range(2)]
         wt_scales = [tile("wt_scales%d" % a, [P, N], U8) for a in range(2)]
@@ -184,36 +218,25 @@ def tile_list_noneP_kernel(
                 mx(y_ps[b][:, t, :], wt_codes[a][:, P * t : P * (t + 1)].bitcast(FP8X4),
                    wt_scales[a][:, P * t : P * (t + 1)], codes, scales, False, last and t == PACK - 1)
 
-        c_first_tier(0)
-        for q in range(1, 4):
-            c_first_tier(q)
-            leftover(q - 1)
-            c_second_tier(q - 1)
-        leftover(3)
-        c_second_tier(3)
-        picked0 = tile("picked0", [P, PACK, J], F32, tag="c_all")
-        gather(0, 0, J, picked0[:, 0, :])
-        wx_sc = tile("wx_sc", [P, N], U8, tag="left_grouped3")
-        nc.vector.tensor_copy(
-            wx_sc[:].rearrange("p (t m) -> p t m", t=PACK),
-            wxs_raw[:].rearrange("p (m t) -> p t m", t=PACK),
-        )
-        for q in range(4):
-            wx_passes(q, wx_sc)
-        gather(1, 0, J, picked0[:, 1, :])
-        xg0_grouped = [tile("xg0_grouped%d" % h, [P, HALF, PACK], BF16) for h in range(2)]
-        for h in range(2):
-            round_pair(xg0_grouped[h], 0, picked0[:, 0:2, h * HALF : (h + 1) * HALF])
-        gather(2, 0, J, picked0[:, 2, :])
-        quantize_wt(0)
-        gather(3, 0, J, picked0[:, 3, :])
-        quantize_wt(1)
-        for h in range(2):
-            round_pair(xg0_grouped[h], 1, picked0[:, 2:4, h * HALF : (h + 1) * HALF])
-        picked1 = tile("picked1", [P, 2, J], F32)
-        gather(4, 0, J, picked1[:, 0, :])
 
-        def first_passes(h):
+        picked0 = tile("picked0", [P, PACK, J], F32, tag="c3")
+        xg0_grouped = [tile("xg0_grouped%d" % h, [P, HALF, PACK], BF16) for h in range(2)]
+        xg1_grouped = [tile("xg1_grouped%d" % q, [P, QUARTER, PACK], BF16) for q in range(4)]
+        y_scales = tile("y_scales", [P, J], U8)
+        y_sb = [tile("y_sb%d" % q, [P, PACK, QUARTER], F32) for q in range(4)]
+        S, V = nc.scalar.copy, nc.vector.tensor_copy
+        st = {}
+
+        def g0(n):
+            gather(n, 0, J, picked0[:, n, :])
+
+        def r0(u, h):
+            round_pair(xg0_grouped[h], u, picked0[:, 2 * u : 2 * u + 2, h * HALF : (h + 1) * HALF])
+
+        def r0full(h):
+            interleave(S, xg0_grouped[h][:], picked0[:, :, h * HALF : (h + 1) * HALF])
+
+        def q0(h):
             codes = tile("xg0_codes%d" % h, [P, HALF], U32)
             scales = tile("xg0_scales%d" % h, [P, HALF], U8)
             quantize(codes[:], scales[:], xg0_grouped[h][:])
@@ -221,46 +244,91 @@ def tile_list_noneP_kernel(
                 cols = slice(u * BANK, (u + 1) * BANK)
                 wt_passes(0, 4 * h + u, codes[:, cols], scales[:, cols], False)
 
-        first_passes(0)
-        gather(5, 0, J, picked1[:, 1, :])
-        first_passes(1)
-        xg1_grouped = [tile("xg1_grouped%d" % q, [P, QUARTER, PACK], BF16) for q in range(4)]
-        for q in range(4):
-            round_pair(xg1_grouped[q], 0, picked1[:, :, q * QUARTER : (q + 1) * QUARTER])
+        def early(q_from, q_to, tag=None):
+            w = (q_to - q_from) * QUARTER
+            t = tile("picked1_%d" % q_from, [P, 2, w], F32, tag=tag)
+            for n in (4, 5):
+                gather(n, q_from * QUARTER, q_to * QUARTER, t[:, n - 4, :])
+            for q in range(q_from, q_to):
+                st[q] = t[:, :, (q - q_from) * QUARTER : (q - q_from + 1) * QUARTER]
 
-        y_scales = tile("y_scales", [P, J], U8)
-        y_sb = [tile("y_sb%d" % q, [P, PACK, QUARTER], F32) for q in range(4)]
+        def r1early(q, copy=S):
+            round_pair(xg1_grouped[q], 0, st[q], copy)
 
-        def last_passes(q):
-            last = tile("picked_last%d" % q, [P, 2, QUARTER], F32, tag="picked_last%d" % (q % 2))
-            gather(6, q * QUARTER, (q + 1) * QUARTER, last[:, 0, :])
-            gather(7, q * QUARTER, (q + 1) * QUARTER, last[:, 1, :])
-            round_pair(xg1_grouped[q], 1, last[:])
+        def last(q, first_plane, copies, tag):
+            t = tile("picked_last%d" % q, [P, 8 - first_plane, QUARTER], F32, tag=tag)
+            for n in range(first_plane, 8):
+                gather(n, q * QUARTER, (q + 1) * QUARTER, t[:, n - first_plane, :])
             codes = tile("xg1_codes%d" % q, [P, QUARTER], U32)
             scales = tile("xg1_scales%d" % q, [P, QUARTER], U8)
-            quantize(codes[:], scales[:], xg1_grouped[q][:])
-            for u in range(2):
-                cols = slice(u * BANK, (u + 1) * BANK)
-                wt_passes(1, 2 * q + u, codes[:, cols], scales[:, cols], True)
+            w = QUARTER // len(copies)
+            for i, copy in enumerate(copies):
+                cols = slice(i * w, (i + 1) * w)
+                if first_plane == 6:
+                    round_pair(xg1_grouped[q][:, cols, :], 1, t[:, :, cols], copy)
+                else:
+                    interleave(copy, xg1_grouped[q][:, cols, :], t[:, :, cols])
+                quantize(codes[:, cols], scales[:, cols], xg1_grouped[q][:, cols, :])
+                for j0 in range(i * w, (i + 1) * w, BANK):
+                    wt_passes(1, 2 * q + j0 // BANK, codes[:, j0 : j0 + BANK], scales[:, j0 : j0 + BANK], True)
 
-        def hand_out(q):
+        def out(q, copies, evac=(S, S)):
             js = slice(q * QUARTER, (q + 1) * QUARTER)
-            for u in range(2):
-                nc.scalar.copy(y_sb[q][:, :, u * BANK : (u + 1) * BANK], y_ps[2 * q + u][:])
-            nc.sync.dma_start(y_rows[:, :, js], y_sb[q][:])
             grouped = tile("y_grouped%d" % q, [P, QUARTER, PACK], BF16)
-            interleave(nc.vector.tensor_copy, grouped[:], y_sb[q][:])
             codes = tile("y_codes%d" % q, [P, QUARTER], U32)
-            quantize(codes[:], y_scales[:, js], grouped[:])
+            w = QUARTER // len(copies)
+            for i, copy in enumerate(copies):
+                cols = slice(i * w, (i + 1) * w)
+                for j0 in range(i * w, (i + 1) * w, BANK):
+                    evac[j0 // BANK](y_sb[q][:, :, j0 : j0 + BANK], y_ps[2 * q + j0 // BANK][:])
+                if i == len(copies) - 1:
+                    nc.sync.dma_start(y_rows[:, :, js], y_sb[q][:])
+                interleave(copy, grouped[:, cols, :], y_sb[q][:, :, cols])
+                quantize(codes[:, cols], y_scales[:, js][:, cols], grouped[:, cols, :])
             nc.sync.dma_start(
                 y_words[:, PACK * q * QUARTER : PACK * (q + 1) * QUARTER].bitcast(I32), codes[:].bitcast(I32)
             )
 
-        last_passes(0)
-        for q in range(1, 4):
-            last_passes(q)
-            hand_out(q - 1)
-        hand_out(3)
+        c_first_tier(0)
+        c_first_tier(1)
+        leftover(0)
+        c_second_tier(0)
+        c_first_tier(2)
+        leftover(1)
+        c_second_tier(1)
+        c_first_tier(3)
+        leftover(2)
+        c_second_tier(2)
+        leftover(3)
+        c_second_tier(3)
+        g0(0)
+        wx_passes(0, wx_sc)
+        wx_passes(1, wx_sc)
+        wx_passes(2, wx_sc)
+        wx_passes(3, wx_sc)
+        g0(1)
+        quantize_wt(0)
+        g0(2)
+        g0(3)
+        quantize_wt(1)
+        r0full(0)
+        r0full(1)
+        early(0,2)
+        early(2,4)
+        q0(0)
+        q0(1)
+        r1early(0)
+        r1early(1)
+        r1early(2)
+        r1early(3)
+        last(0,6,[S],'a')
+        last(1,6,[S],'b')
+        out(0,[V])
+        last(2,6,[S],'a')
+        out(1,[V])
+        last(3,6,[V,V],'b')
+        out(2,[V])
+        out(3,[V,V])
         for q in range(4):
             queue = nc.sync if q % 2 == 0 else nc.scalar
             queue.dma_start(

@@ -81,10 +81,10 @@ def tile_list_noneP_kernel(
         nc.sync.dma_start(wgt_sb[:], wgt)
         load_x(0)
         load_x(1)
-        load_wt(0)
         load_x(2)
-        load_wt(1)
+        load_wt(0)
         load_x(3)
+        load_wt(1)
         load_x(4)
         load_x(5)
         load_x(6)
@@ -129,7 +129,7 @@ def tile_list_noneP_kernel(
                     b = 2 * q + u
                     cols = slice(u * BANK, (u + 1) * BANK)
                     if first:
-                        y_ps[b] = ps.tile([P, PACK, BANK], F32, name="y%d" % b, tag="bank%d" % (7 - b))
+                        y_ps[b] = ps.tile([P, PACK, BANK], F32, name="y%d" % b, tag="bank%d" % b)
                     for t in range(PACK):
                         mx(y_ps[b][:, t, :], wx_codes[:, 2 * P * t : 2 * P * (t + 1)].bitcast(FP4X4),
                            wx_sc[:, P * t : P * (t + 1)], codes[:, cols], scales[:, cols], first and t == 0, False)
@@ -219,8 +219,9 @@ def tile_list_noneP_kernel(
                    wt_scales[a][:, P * t : P * (t + 1)], codes, scales, False, last and t == PACK - 1)
 
 
-        picked0 = tile("picked0", [P, PACK, J], F32, tag="c3")
-        xg0_grouped = [tile("xg0_grouped%d" % h, [P, HALF, PACK], BF16) for h in range(2)]
+        picked0 = tile("picked0", [P, PACK, J], F32, tag="c1")
+        xg0_all = tile("xg0_grouped", [P, J, PACK], BF16, tag="wt1")
+        xg0_grouped = [xg0_all[:, h * HALF : (h + 1) * HALF, :] for h in range(2)]
         xg1_grouped = [tile("xg1_grouped%d" % q, [P, QUARTER, PACK], BF16) for q in range(4)]
         y_scales = tile("y_scales", [P, J], U8)
         y_sb = [tile("y_sb%d" % q, [P, PACK, QUARTER], F32) for q in range(4)]
@@ -233,8 +234,8 @@ def tile_list_noneP_kernel(
         def r0(u, h):
             round_pair(xg0_grouped[h], u, picked0[:, 2 * u : 2 * u + 2, h * HALF : (h + 1) * HALF])
 
-        def r0full(h):
-            interleave(S, xg0_grouped[h][:], picked0[:, :, h * HALF : (h + 1) * HALF])
+        def r0full(h, copy=S):
+            interleave(copy, xg0_grouped[h][:], picked0[:, :, h * HALF : (h + 1) * HALF])
 
         def q0(h):
             codes = tile("xg0_codes%d" % h, [P, HALF], U32)
@@ -297,36 +298,34 @@ def tile_list_noneP_kernel(
         leftover(1)
         c_second_tier(1)
         c_first_tier(3)
-        leftover(2)
-        c_second_tier(2)
-        leftover(3)
-        c_second_tier(3)
+        leftover_on_tensor(2)
+        leftover_on_tensor(3)
         g0(0)
         wx_passes(0, wx_sc)
         wx_passes(1, wx_sc)
+        g0(1)
+        g0(2)
+        c_second_tier(2)
+        c_second_tier(3)
         wx_passes(2, wx_sc)
         wx_passes(3, wx_sc)
-        g0(1)
         quantize_wt(0)
-        g0(2)
         g0(3)
         quantize_wt(1)
         r0full(0)
         r0full(1)
-        early(0,2)
-        early(2,4)
+        early(0,3)
         q0(0)
         q0(1)
         r1early(0)
         r1early(1)
         r1early(2)
-        r1early(3)
         last(0,6,[S],'a')
         last(1,6,[S],'b')
-        out(0,[V])
+        out(0,[S])
         last(2,6,[S],'a')
         out(1,[V])
-        last(3,6,[V,V],'b')
+        last(3,4,[S,V],'b')
         out(2,[V])
         out(3,[V,V])
         for q in range(4):

from contextlib import ExitStack

import concourse.mybir as mybir
from concourse.masks import make_identity

K, L, N, T, J = 1024, 512, 512, 2048, 1024
FLOPS = 2 * (K * N * J + 2 * L * N * J + L * L * J)

F32 = mybir.dt.float32
BF16 = mybir.dt.bfloat16
I32 = mybir.dt.int32
U32 = mybir.dt.uint32
U16 = mybir.dt.uint16
U8 = mybir.dt.uint8
FP8X4 = mybir.dt.float8_e4m3fn_x4
FP4X4 = mybir.dt.float4_e2m1fn_x4
MULT = mybir.AluOpType.mult
SUB = mybir.AluOpType.subtract

P = 128
PACK = 4
BANK = 128
HALF = 512
QUARTER = 256


def tile_list_noneP_kernel(
    tc, xT, wgt, wt, c, wx_words, wx_scales, offs, out_0, out_1, out_2
):
    nc = tc.nc
    with ExitStack() as ctx:
        sb = ctx.enter_context(tc.tile_pool(name="sb", bufs=1))
        ps = ctx.enter_context(tc.psum_pool(name="ps", bufs=1))

        def tile(name, shape, dtype, tag=None):
            return sb.tile(shape, dtype, name=name, tag=tag or name, align_bytes=64)

        def quantize(codes, scales, grouped):
            nc.vector.quantize_mx(
                out=codes.bitcast(FP8X4), scales=scales, in_=grouped.rearrange("p w i -> p (w i)")
            )

        def interleave(copy, grouped, planes):
            copy(
                grouped.rearrange("p (g e) i -> p g i e", e=4),
                planes.rearrange("p i (g e) -> p g i e", e=4),
            )

        x_rows = xT.rearrange("(a p i) t -> a i p t", p=P, i=PACK)
        wt_rows = wt.rearrange("(a p i) n -> a p i n", p=P, i=PACK)
        c_rows = c.rearrange("(p i) j -> p i j", i=PACK)
        y_rows = out_0.rearrange("(p i) j -> p i j", i=PACK)
        y_words = out_1[0].rearrange("p j i -> p (j i)")

        offsets = tile("offsets", [P, J // 16], U16)
        c_sb = [tile("c%d" % q, [P, PACK, QUARTER], F32) for q in range(4)]
        wgt_sb = tile("wgt", [P, J], F32)
        x_sb = [tile("x%d" % n, [P, T], F32) for n in range(8)]
        wt_sb = [tile("wt%d" % a, [P, PACK, N], F32) for a in range(2)]
        wx_raw = tile("wx_raw", [P, 2 * N], U8)
        wxs_raw = tile("wxs_raw", [P, N], U8)

        def load_x(n):
            nc.sync.dma_start(x_sb[n][:], x_rows[n // PACK, n % PACK])

        def load_c(q):
            nc.sync.dma_start(c_sb[q][:], c_rows[:, :, q * QUARTER : (q + 1) * QUARTER])

        def load_wt(a):
            nc.sync.dma_start(wt_sb[a][:], wt_rows[a])

        nc.sync.dma_start(wx_raw[:].bitcast(I32), wx_words[0].bitcast(I32))
        load_c(0)
        for q in range(4):
            rows = wx_scales[:, 4 * q : 4 * q + 4, :].bitcast(I32)
            nc.sync.dma_start(wxs_raw[32 * q : 32 * (q + 1), :].bitcast(I32), rows.broadcast_to([8, 4, N // 4]))
        load_c(1)
        load_c(2)
        load_c(3)
        nc.sync.dma_start(offsets[:], offs)
        nc.sync.dma_start(wgt_sb[:], wgt)
        load_x(0)
        load_x(1)
        load_x(2)
        load_wt(0)
        load_x(3)
        load_wt(1)
        load_x(4)
        load_x(5)
        load_x(6)
        load_x(7)

        eye = tile("eye", [P, P], F32)
        make_identity(nc, eye[:])
        eye_flat = tile("eye_grouped", [P, PACK * (PACK * P + 1)], BF16)
        nc.gpsimd.memset(eye_flat[:].bitcast(U32), 0)
        diagonals = eye_flat[:].rearrange("p (t w) -> p t w", t=PACK)[:, :, 0 : PACK * P : PACK]
        nc.scalar.copy(diagonals, eye[:].unsqueeze(1).broadcast_to([P, PACK, P]))
        eye_codes = tile("eye_codes", [P, PACK * P], U32)
        eye_scales = tile("eye_scales", [P, PACK * P], U8)
        nc.vector.quantize_mx(out=eye_codes[:].bitcast(FP8X4), scales=eye_scales[:], in_=eye_flat[:, 0 : PACK * PACK * P])

        wx_codes = tile("wx_codes", [P, 2 * N], U8)
        nc.vector.tensor_copy(
            wx_codes[:].bitcast(U16).rearrange("p (t m) -> p t m", t=PACK),
            wx_raw[:].bitcast(U16).rearrange("p (m t) -> p t m", t=PACK),
        )
        wx_sc = tile("wx_sc", [P, N], U8)
        nc.vector.tensor_copy(
            wx_sc[:].rearrange("p (t m) -> p t m", t=PACK),
            wxs_raw[:].rearrange("p (m t) -> p t m", t=PACK),
        )

        cq_codes = [tile("cq_codes%d" % q, [P, QUARTER], U32) for q in range(4)]
        cq_scales = [tile("cq_scales%d" % q, [P, QUARTER], U8) for q in range(4)]
        cr_codes = [tile("cr_codes%d" % q, [P, QUARTER], U32) for q in range(4)]
        cr_scales = [tile("cr_scales%d" % q, [P, QUARTER], U8) for q in range(4)]
        y_ps = {}

        def mx(out, w_codes, w_scales, m_codes, m_scales, start, stop):
            nc.tensor.matmul_mx(
                out=out, lhsT=w_codes, lhsT_scale=w_scales, rhs=m_codes.bitcast(FP8X4), rhs_scale=m_scales,
                start=start, stop=stop,
            )

        def wx_passes(q, wx_sc):
            for codes, scales, first in ((cr_codes[q], cr_scales[q], True), (cq_codes[q], cq_scales[q], False)):
                for u in range(2):
                    b = 2 * q + u
                    cols = slice(u * BANK, (u + 1) * BANK)
                    if first:
                        y_ps[b] = ps.tile([P, PACK, BANK], F32, name="y%d" % b, tag="bank%d" % b)
                    for t in range(PACK):
                        mx(y_ps[b][:, t, :], wx_codes[:, 2 * P * t : 2 * P * (t + 1)].bitcast(FP4X4),
                           wx_sc[:, P * t : P * (t + 1)], codes[:, cols], scales[:, cols], first and t == 0, False)

        back = {}

        c_grouped = tile("c_grouped", [P, J, PACK], BF16, tag="eye_grouped")

        def c_first_tier(q):
            grouped = c_grouped[:, q * QUARTER : (q + 1) * QUARTER, :]
            interleave(nc.scalar.copy, grouped, c_sb[q][:])
            quantize(cq_codes[q][:], cq_scales[q][:], grouped)
            for u in range(2):
                b = 2 * q + u
                cols = slice(u * BANK, (u + 1) * BANK)
                back[b] = ps.tile([P, PACK, BANK], F32, name="back%d" % b, tag="bank%d" % b)
                for t in range(PACK):
                    mx(back[b][:, t, :], eye_codes[:, P * t : P * (t + 1)].bitcast(FP8X4),
                       eye_scales[:, P * t : P * (t + 1)], cq_codes[q][:, cols], cq_scales[q][:, cols], True, True)

        left = {}

        def leftover(q):
            left[q] = tile("left_grouped%d" % q, [P, QUARTER, PACK], BF16)[:]
            for u in range(2):
                cols = slice(u * BANK, (u + 1) * BANK)
                nc.vector.tensor_tensor(
                    left[q][:, cols, :].rearrange("p (g e) i -> p g i e", e=4),
                    c_sb[q][:, :, cols].rearrange("p i (g e) -> p g i e", e=4),
                    back[2 * q + u][:].rearrange("p i (g e) -> p g i e", e=4),
                    SUB,
                )

        def leftover_on_tensor(q):
            flat = tile("left_grouped%d" % q, [P, QUARTER * PACK], BF16)
            left[q] = flat[:].rearrange("p (j i) -> p j i", i=PACK)
            for u in range(2):
                b = 2 * q + u
                cols = slice(u * BANK, (u + 1) * BANK)
                negated = tile("negated%d" % b, [P, PACK, BANK], F32)
                nc.scalar.mul(negated[:], back[b][:], -1.0)
                turned = ps.tile([P, PACK, P], F32, name="turned%d" % b, tag="bank%d" % b)
                for t in range(PACK):
                    nc.tensor.matmul(turned[:, t, :], lhsT=c_sb[q][:, t, cols], rhs=eye[:], is_transpose=True,
                                     start=t == 0, stop=False)
                for t in range(PACK):
                    nc.tensor.matmul(turned[:, t, :], lhsT=negated[:, t, :], rhs=eye[:], is_transpose=True,
                                     start=False, stop=t == PACK - 1)
                rounded = tile("rounded%d" % b, [P, PACK * P], BF16)
                nc.scalar.copy(
                    rounded[:].rearrange("j (v p e) -> j v p e", v=2, e=2),
                    turned[:].rearrange("j (v e) p -> j v p e", v=2),
                )
                pairs = ps.tile([P, 2, BANK], F32, name="pairs%d" % b, tag="bank%d" % b)
                for v in range(2):
                    nc.tensor.transpose(pairs[:, v, :], rounded[:].bitcast(F32)[:, v * P : (v + 1) * P], eye[:])
                nc.scalar.copy(
                    flat[:].bitcast(F32)[:, 2 * u * BANK : 2 * (u + 1) * BANK].rearrange("p (j v) -> p j v", v=2),
                    pairs[:].rearrange("p v j -> p j v"),
                )

        def c_second_tier(q):
            quantize(cr_codes[q][:], cr_scales[q][:], left[q])

        def gather(n, j0, j1, dst):
            nc.vector.tensor_tensor(
                dst, x_sb[n][:].indirect(offsets[:, j0 // 16 : j1 // 16]), wgt_sb[:, j0:j1], MULT
            )

        def round_pair(grouped, u, src, copy=nc.scalar.copy):
            copy(grouped[:, :, 2 * u : 2 * u + 2], src.rearrange("p e j -> p j e"))

        wt_codes = [tile("wt_codes%d" % a, [P, N], U32) for a in range(2)]
        wt_scales = [tile("wt_scales%d" % a, [P, N], U8) for a in range(2)]

        def quantize_wt(a):
            grouped = tile("wt_grouped%d" % a, [P, N, PACK], BF16)
            nc.scalar.copy(
                grouped[:].rearrange("p (t m) i -> p m i t", t=PACK),
                wt_sb[a][:].rearrange("p i (m t) -> p m i t", t=PACK),
            )
            quantize(wt_codes[a][:], wt_scales[a][:], grouped[:])

        def wt_passes(a, b, codes, scales, last):
            for t in range(PACK):
                mx(y_ps[b][:, t, :], wt_codes[a][:, P * t : P * (t + 1)].bitcast(FP8X4),
                   wt_scales[a][:, P * t : P * (t + 1)], codes, scales, False, last and t == PACK - 1)


        picked0 = tile("picked0", [P, PACK, J], F32, tag="c1")
        xg0_all = tile("xg0_grouped", [P, J, PACK], BF16, tag="wt1")
        xg0_grouped = [xg0_all[:, h * HALF : (h + 1) * HALF, :] for h in range(2)]
        xg1_grouped = [tile("xg1_grouped%d" % q, [P, QUARTER, PACK], BF16) for q in range(4)]
        y_scales = tile("y_scales", [P, J], U8)
        y_sb = [tile("y_sb%d" % q, [P, PACK, QUARTER], F32) for q in range(4)]
        S, V = nc.scalar.copy, nc.vector.tensor_copy
        st = {}

        def g0(n):
            gather(n, 0, J, picked0[:, n, :])

        def r0(u, h):
            round_pair(xg0_grouped[h], u, picked0[:, 2 * u : 2 * u + 2, h * HALF : (h + 1) * HALF])

        def r0full(h, copy=S):
            interleave(copy, xg0_grouped[h][:], picked0[:, :, h * HALF : (h + 1) * HALF])

        def q0(h):
            codes = tile("xg0_codes%d" % h, [P, HALF], U32)
            scales = tile("xg0_scales%d" % h, [P, HALF], U8)
            quantize(codes[:], scales[:], xg0_grouped[h][:])
            for u in range(4):
                cols = slice(u * BANK, (u + 1) * BANK)
                wt_passes(0, 4 * h + u, codes[:, cols], scales[:, cols], False)

        def early(q_from, q_to, tag=None):
            w = (q_to - q_from) * QUARTER
            t = tile("picked1_%d" % q_from, [P, 2, w], F32, tag=tag)
            for n in (4, 5):
                gather(n, q_from * QUARTER, q_to * QUARTER, t[:, n - 4, :])
            for q in range(q_from, q_to):
                st[q] = t[:, :, (q - q_from) * QUARTER : (q - q_from + 1) * QUARTER]

        def r1early(q, copy=S):
            round_pair(xg1_grouped[q], 0, st[q], copy)

        def last(q, first_plane, copies, tag):
            t = tile("picked_last%d" % q, [P, 8 - first_plane, QUARTER], F32, tag=tag)
            for n in range(first_plane, 8):
                gather(n, q * QUARTER, (q + 1) * QUARTER, t[:, n - first_plane, :])
            codes = tile("xg1_codes%d" % q, [P, QUARTER], U32)
            scales = tile("xg1_scales%d" % q, [P, QUARTER], U8)
            w = QUARTER // len(copies)
            for i, copy in enumerate(copies):
                cols = slice(i * w, (i + 1) * w)
                if first_plane == 6:
                    round_pair(xg1_grouped[q][:, cols, :], 1, t[:, :, cols], copy)
                else:
                    interleave(copy, xg1_grouped[q][:, cols, :], t[:, :, cols])
                quantize(codes[:, cols], scales[:, cols], xg1_grouped[q][:, cols, :])
                for j0 in range(i * w, (i + 1) * w, BANK):
                    wt_passes(1, 2 * q + j0 // BANK, codes[:, j0 : j0 + BANK], scales[:, j0 : j0 + BANK], True)

        def out(q, copies, evac=(S, S)):
            js = slice(q * QUARTER, (q + 1) * QUARTER)
            grouped = tile("y_grouped%d" % q, [P, QUARTER, PACK], BF16)
            codes = tile("y_codes%d" % q, [P, QUARTER], U32)
            w = QUARTER // len(copies)
            for i, copy in enumerate(copies):
                cols = slice(i * w, (i + 1) * w)
                for j0 in range(i * w, (i + 1) * w, BANK):
                    evac[j0 // BANK](y_sb[q][:, :, j0 : j0 + BANK], y_ps[2 * q + j0 // BANK][:])
                if i == len(copies) - 1:
                    nc.sync.dma_start(y_rows[:, :, js], y_sb[q][:])
                interleave(copy, grouped[:, cols, :], y_sb[q][:, :, cols])
                quantize(codes[:, cols], y_scales[:, js][:, cols], grouped[:, cols, :])
            nc.sync.dma_start(
                y_words[:, PACK * q * QUARTER : PACK * (q + 1) * QUARTER].bitcast(I32), codes[:].bitcast(I32)
            )

        c_first_tier(0)
        c_first_tier(1)
        leftover(0)
        c_second_tier(0)
        c_first_tier(2)
        leftover(1)
        c_second_tier(1)
        c_first_tier(3)
        leftover_on_tensor(2)
        leftover_on_tensor(3)
        g0(0)
        wx_passes(0, wx_sc)
        wx_passes(1, wx_sc)
        g0(1)
        g0(2)
        c_second_tier(2)
        c_second_tier(3)
        wx_passes(2, wx_sc)
        wx_passes(3, wx_sc)
        quantize_wt(0)
        g0(3)
        quantize_wt(1)
        r0full(0)
        r0full(1)
        early(0,3)
        q0(0)
        q0(1)
        r1early(0)
        r1early(1)
        r1early(2)
        last(0,6,[S],'a')
        last(1,6,[S],'b')
        out(0,[S])
        last(2,6,[S],'a')
        out(1,[V])
        last(3,4,[S,V],'b')
        out(2,[V])
        out(3,[V,V])
        for q in range(4):
            queue = nc.sync if q % 2 == 0 else nc.scalar
            queue.dma_start(
                out_2[0, 4 * q : 4 * q + 4, :].bitcast(I32), y_scales[32 * q : 32 * q + 4, :].bitcast(I32)
            )
